import numpy as np, ml_dtypes
CORES = [1,5,17,21,33,37,49,53]
N = 8
import mx_ref
BF = ml_dtypes.bfloat16
def gentries(a):
    return np.ascontiguousarray(a.reshape(8, 16, -1).transpose(0, 2, 1)).reshape(8, -1)
def gtable(e):
    e = np.asarray(e); return np.ascontiguousarray(e.reshape(8, -1, 16).transpose(0, 2, 1)).reshape(128, -1).astype(np.int32)
def gcols(t, e):
    v = np.concatenate([t.reshape(8, 16, -1, 4), np.zeros((8, 16, 1, 4), BF)], axis=2)
    return np.ascontiguousarray(np.stack([v[g][:, e[g]] for g in range(8)])).reshape(128, -1)
def tile(rs):
    return np.stack(rs, axis=2).reshape(128, -1).astype(BF)
def pick(q, e):
    c = np.concatenate([q[0].reshape(128, -1, 4), np.zeros((128, 1, 4), np.uint8)], axis=1); s = np.concatenate([q[1], np.ones((16, 1), np.uint8)], axis=1)
    return (np.ascontiguousarray(c[:, e].reshape(128, -1)), np.ascontiguousarray(s[:, e]))
def join(*qs):
    return (np.concatenate([q[0] for q in qs], axis=1), np.concatenate([q[1] for q in qs], axis=1))
def put(q, e, v):
    c, s = q[0].reshape(128, -1, 4).copy(), q[1].copy(); c[:, e] = v[0].reshape(128, -1, 4); s[:, e] = v[1]
    return (c.reshape(128, -1), s)
def pk(c, s):
    return (np.ascontiguousarray(c), mx_ref.live(s))
def emit(q):
    return q[0], q[1]
def packed(v, rng):
    q = [mx_ref.quantize(np.ascontiguousarray(v[r])) for r in range(N)]
    return np.stack([a for a, b in q]), np.stack([mx_ref.plane(b, rng) for a, b in q])
def values_of_codes():
    e, c = np.zeros((128, 128, 4), np.float32), np.zeros((128, 2, 4), np.uint8)
    e[np.arange(128), np.arange(128), 0] = 1
    c[:127, :, 0] = np.arange(256).reshape(2, 128).T[:127]
    return mx_ref.matmul(mx_ref.quantize(e.reshape(128, 512).astype(BF)), (c.reshape(128, 8), np.full((16, 2), 127, np.uint8))).T.reshape(-1).astype(np.float64)
CODE_VALUE, SCALE_VALUE = values_of_codes(), 2.0 ** (np.arange(256) - 127.0)
def decode(q):
    return (CODE_VALUE[q[0]].reshape(16, 8, -1, 4) * SCALE_VALUE[q[1]][:, None, :, None] + 0.0).reshape(128, -1).astype(np.float32)
def f(rng, *shape):
    return mx_ref.flush((rng.standard_normal(shape, dtype=np.float32) * np.exp2(rng.integers(-2, 3, shape[:-1] + (1,)))).astype(BF))
def wide(rng, *shape, cols=0):
    v = rng.standard_normal(shape, dtype=np.float32) * np.exp2(rng.integers(-12, 13, shape)).astype(np.float32)
    if cols: v *= np.repeat(np.exp2(rng.integers(-cols, cols + 1, shape[:-2] + (1, shape[-1] // 4))) * (rng.random(shape[:-2] + (1, shape[-1] // 4)) > 0.0625), 4, axis=-1).astype(np.float32)
    return mx_ref.flush(v.astype(BF))
C, E, R = 256, 256, 3
def parts(m):
    return np.repeat(np.repeat(m, 16, axis=0), 4, axis=1)
def big(v):
    v = v.astype(np.float32)
    v[np.abs(v) < np.float32(2.0 ** -16)] = 0
    return v.astype(BF)
def numbers_of(rng):
    return {"x": big(f(rng, N, 128, 4 * C)), "u": np.array(f(rng, N, 128, 512)), "v": np.array(f(rng, N, 128, 512))}
def layer(rng, still=0):
    w = big(f(rng, N, 128, 2048)).reshape(N, 8, 16, 4, 8, 16, 4)
    w[:, :, :, :, :, :still] = 0
    return w
def moved(rng, rows):
    w = np.zeros((N, 128, 4, 128, 4), np.float32)
    for r in range(N):
        h, e = 16 * rng.integers(8), rng.integers(4)
        for b in range(4): w[r, (rows + h) % 128, b, rows, (b + e) % 4] = rng.choice([-16.0, 16.0], len(rows))
    return w.astype(BF)
def weights(rng, w, m):
    wc, ws = packed(np.ascontiguousarray(w).reshape(N, 128, 2048), rng)
    mc, ms = packed(np.ascontiguousarray(m).reshape(N, 128, 2048), rng)
    return {"wc": wc, "ws": ws, "mc": mc, "ms": ms}
def orders(rng):
    return np.argsort(rng.random((N, 8, 2 * R, C)), axis=3)
def lists(e):
    return np.stack([gtable(e[r].reshape(8, -1)) for r in range(N)])
def signs(rng):
    return np.stack([rng.permutation(8) % 2 * 2.0 - 1.0 for r in range(N)])
def setup_inputs(rng):
    return {**numbers_of(rng), **weights(rng, layer(rng), layer(rng)), "pl": lists(orders(rng))}
def setup_inputs_ties(rng):
    d = numbers_of(rng)
    e = rng.permutation(N)
    x = d["x"].reshape(N, 8, 16, C, 4)
    for r in range(N):
        k = np.zeros(C, int) if r == e[0] else rng.permutation(C) % 3
        a = x[r][:, :8, :3].copy()
        a[:, :, 2] = 0
        x[r][:, :8] = a[:, :, k]
    x[e[1], :, :8] = 0
    u = d["u"].reshape(N, 8, 16, 128, 4)
    for k in range(3): u[:, :, 8:, k::16] = 0
    return {"x": x.reshape(N, 128, 4 * C), "u": u.reshape(N, 128, 512), "v": d["v"], **weights(rng, layer(rng, 8), layer(rng, 8)), "pl": lists(orders(rng))}
def setup_inputs_near(rng):
    d = numbers_of(rng)
    x = np.zeros((N, 8, 16, C, 4), np.float32)
    u = d["u"].reshape(N, 128, 128, 4)
    for k in range(3): u[:, :, k::16] = 0
    o = rng.permutation(N) % 4
    c = [signs(rng), signs(rng)]
    j = np.arange(C)
    for r in range(N):
        size, one = (1.0, 1.0) if o[r] < 2 else (2.0 ** -4, 2.0 ** -27)
        for k in range(2):
            a = np.where(rng.permutation(8) % 2 == 0, E - 1, rng.integers(0, E, 8))[:, None]
            s = ((j + a) % E + rng.integers(0, 2, (8, 1))) // 2
            s[:, E:] = E // 2 + 1
            g = ((s[:, :, None] >> np.arange(8)) & 1) * np.exp2(np.arange(8) - 23.0) * size
            top = E - 1 - rng.integers(0, E // 8, (8, 1))
            if o[r] == 3:
                high = (j == top) | (j == 0) | (j >= E)
                x[r, :, k, :, 0] = (8 + high) * 2.0 ** -30
                x[r, :, 4 + k, :, 0] = (9 - high) * 2.0 ** -30
            else:
                if o[r] < 2: x[r, :, k, :, 0] = c[k][r][:, None]
                x[r, :, 8 + 2 * k] = g[:, :, :4]
                x[r, :, 9 + 2 * k] = g[:, :, 4:]
        x[r, :, 2, :, 0] = rng.integers(-1, 2, (8, C)) * one
        if o[r] == 2:
            x[r, :, 3] = x[r, :, 2]
            x[r, :, 2] *= 1.125
        if o[r] == 3:
            for g in rng.permutation(8)[:4]: x[r, g, 2, :, 0] = one
        x[r, :, 12:] = rng.integers(4, 8, (8, 4, C, 4)) * rng.choice([-1.0, 1.0], (8, 4, C, 4)) * 2.0 ** -20
        z = 1.0 if o[r] == 0 else 2.0 ** -30
        for h in range(0, 128, 16):
            for k in range(3): u[r, h + k, h + k, 0] = z
            for k in range(2): u[r, h + 8 + 2 * k:h + 10 + 2 * k, h + k] = z
            if o[r] == 2: u[r, h + 3, h + 2, 0] = -z
            if o[r] == 3:
                for k in range(2):
                    u[r, h + k, h + k, 0] = 1.125 * z
                    u[r, h + 4 + k, h + k, 0] = z
    rows = np.flatnonzero(np.arange(128) % 16 >= 12)
    return {"x": x.reshape(N, 128, 4 * C).astype(BF), "u": u.reshape(N, 128, 512), "v": d["v"], **weights(rng, moved(rng, rows), moved(rng, rows)), "pl": lists(orders(rng))}
def setup_inputs_huge(rng):
    d = numbers_of(rng)
    c = np.ones((N, C))
    for r in rng.permutation(N)[:N // 2]: c[r] = rng.permutation(C) % 2 * 2.0 - 1.0
    x = 2.0 ** 30 * (0.8 + 0.2 * rng.random((N, 128, C, 4))) * c[:, None, :, None]
    u = d["u"].reshape(N, 128, 8, 16, 4)
    a = 2.0 ** 30 * (1 - 0.1 * rng.random((N, 128, 8, 3, 4))) * np.stack([signs(rng), signs(rng), signs(rng)], axis=2)[:, None, :, :, None]
    u[:, :, :, :3] = a.astype(np.float32).astype(BF)
    rows = np.arange(128)
    return {"x": x.astype(np.float32).reshape(N, 128, 4 * C).astype(BF), "u": u.reshape(N, 128, 512), "v": d["v"], **weights(rng, moved(rng, rows), moved(rng, rows)), "pl": lists(orders(rng))}
def setup_inputs_places(rng):
    d = numbers_of(rng)
    x = d["x"].reshape(N, 8, 16, C, 4)
    x[:, :, :8] = 0
    u = d["u"].reshape(N, 128, 128, 4)
    for k in range(3): u[:, :, k::16] = 0
    for h in range(0, 128, 16):
        for k in range(3): u[:, h + k, h + k, 0] = 1
    e = orders(rng)
    for r in range(N):
        b = [rng.permutation(np.array([1, 2, E // 2 - 1, E // 2, E // 2 + 1, E - 1, rng.integers(1, E), rng.integers(1, E)])) for k in range(2)]
        same, kinds = rng.permutation(8)[:4], rng.permutation(8)
        b[1][same] = b[0][same]
        for g in range(8):
            for k in range(2):
                s = rng.integers(8, 16, C) * 0.0625
                s[0], s[E:], s[b[k][g]] = 4, 4, 2
                x[r, g, k, :, 0] = s
            s = rng.integers(-1, 2, C)
            if kinds[g] < 3: s[:] = kinds[g] - 1
            if kinds[g] == 3: s = (np.arange(C) == rng.integers(C)) * 2 - 1
            x[r, g, 2, :, 0] = s
        for i in range(2 * R):
            h = (r + i) % 4
            if h == 0: e[r, :, i] = np.arange(C)
            if h == 1: e[r, :, i] = np.arange(C)[::-1]
            if h == 2: e[r, :, i] = e[r, 0, i].copy()
    return {"x": x.reshape(N, 128, 4 * C), "u": u.reshape(N, 128, 512), "v": d["v"], **weights(rng, layer(rng, 8), layer(rng, 8)), "pl": lists(e)}
def setup_inputs_spread(rng):
    d = setup_inputs(rng)
    d["x"] = big(wide(rng, N, 128, 4 * C, cols=6))
    return d
def check_inputs(d):
    b = []
    for k in ("x", "u", "v"):
        a = np.abs(d[k].astype(np.float32))
        if not (np.isfinite(a).all() and ((a == 0) | (a >= 2.0 ** -30) & (a <= 2.0 ** 30)).all()): b.append("a value of " + k)
    none, least, most = [emit(mx_ref.quantize(np.full((128, 16), k, np.float32).astype(BF)))[1][0, 0] for k in (0.0, 2.0 ** -30, 2.0 ** 30)]
    for c, s in (("wc", "ws"), ("mc", "ms")):
        if ((d[c] & 0x7F) == 0x7F).any(): b.append("a code of " + c + " that is no number")
        for r in range(N):
            a = mx_ref.live(d[s][r])
            if ((a != none) & ((a < least) | (a > most))).any(): b.append("a scale of " + s)
    for r in range(N):
        e = gentries(d["pl"][r]).reshape(8, 2 * R, C)
        if not (np.sort(e, axis=2) == np.arange(C)).all(): b.append("a list of pl that is no permutation")
    return b
def reference(x, u, v, wc, ws, mc, ms, pl):
    qu = [mx_ref.quantize(u[r]) for r in range(N)]
    lay = [[pk(wc[r], ws[r]), pk(mc[r], ms[r])] for r in range(N)]
    at = [gentries(pl[r]).reshape(8, 2 * R, C) for r in range(N)]
    now = [x[r] for r in range(N)]
    place = np.arange(C)
    od = np.zeros((N, 8, 2 * R), np.float32)
    for t in range(R):
        for r in range(N):
            far = (r + 1 + t) % N
            q = mx_ref.quantize(now[r])
            s = mx_ref.matmul(qu[r], q) + np.float32(0.0)
            turn = np.where(parts(s[2::16] > 0), np.float32(1.0), np.float32(-1.0))
            fold = (decode(q) * turn).astype(BF)
            own = now[r].astype(np.float32) * turn
            back = []
            for k in range(2):
                b = 1 + np.argmax(s[k::16, 1:E], axis=1)
                od[r, :, 2 * t + k] = b
                low = np.stack([place[place < place ^ j] for j in b])
                i = np.take_along_axis(at[r][:, 2 * t + k], low, axis=1)
                m = np.take_along_axis(at[r][:, 2 * t + k], low ^ b[:, None], axis=1)
                z = mx_ref.quantize(((gcols(fold, i).astype(np.float32) + gcols(fold, m).astype(np.float32)) * np.float32(0.5)).astype(BF))
                h = mx_ref.quantize(tile([mx_ref.matmul(pick(lay[far][k], np.arange(128 * j, 128 * j + 128)), z) * np.float32(0.03125) for j in range(4)]))
                n = np.zeros((8, C), int)
                for e in (i, m): np.put_along_axis(n, e, np.broadcast_to(np.arange(C // 2), (8, C // 2)), axis=1)
                back.append(gcols(decode(h).astype(BF), n).astype(np.float32))
            middle = np.maximum(np.minimum(back[0], back[1]), np.minimum(np.maximum(back[0], back[1]), own))
            now[r] = ((own + middle) * np.float32(0.5)).astype(BF)
    y = np.zeros((N, 128, C), np.float32)
    oc, osc = np.zeros((N, 128, 4 * C), np.uint8), np.zeros((N, 16, C), np.uint8)
    for r in range(N):
        q = mx_ref.quantize(now[r])
        y[r] = mx_ref.matmul(mx_ref.quantize(v[r]), q)
        oc[r], osc[r] = emit(q)
    return {"y": y, "od": od, "oc": oc, "osc": osc}

from concourse.mybir import dt, AluOpType as ALU, ActivationFunctionType as AF

F32, BF, I32, U16, U8, MX = "float32", "bfloat16", "int32", "uint16", "uint8", "float8_e4m3fn_x4"
R = 3
BIG = 1e29
KEEP = 4096.0
ROW = 272
HS = 4 * ROW

SCRATCH = {"p0": ("psum", [128, 2048], F32), "p1": ("psum", [128, 2048], F32)}
for _d, _l in (
    (BF, "xt 1024 ub 512 vb 512 ev 520 ea 520 eb 1032 dl 544 tab 2176 a4 512 a16 512 io4 256 io8 256 ion 256 neg 256 ioe 256 "
         "e4 512 gu 512 junk 256 junk2 16 tt 256 sc2 512 sc3 256 n1 256 sn 512 sns 512 xw 2048 ys 1024 yn 1024 dw 2048 "
         "zi 1024 zt 1024 ht 1024 d1 512 ma 2048 mb 2048 mm 2048"),
    (F32, "cf 24 rows 64 two 32 hrow 16 am 72 oy 192 run 256 cnt 8 er 512 gr 512 sc 512 bg 48 bo 6 yo 256"),
    (I32, "pli 96 pi 1 ci 8"),
    (U16, "plu 96 ao 64 uo 16 offu 2 alist 32 l16 32 off 64 ofd 64 ofy 64 bu 4 of0 128 of1 128 of2 128 lo0 128 lo1 128 lo2 128"),
    (MX, "wq 1024 uq 128 uq2 256 vq 128 eq 512 zq 256 xq3 256"),
    (U8, "wp 1024 up 128 up2 256 vp 128 ep 512 zp 256 xp3 256"),
):
    _w = _l.split()
    for _i in range(0, len(_w), 2):
        SCRATCH[_w[_i]] = ("sbuf", [128, int(_w[_i + 1])], _d)
for _t in range(R):
    for _n in ("xq", "lx", "hq", "lh"):
        SCRATCH["%s%d" % (_n, _t)] = ("sbuf", [128, 256], MX)
    for _n in ("xp", "lp", "hp", "lhp"):
        SCRATCH["%s%d" % (_n, _t)] = ("sbuf", [128, 256], U8)

SEMAPHORES = ["qv", "qa", "qp", "qg", "ldx", "ldu", "ldl", "ldw", "ldv"]
for _t in range(R):
    SEMAPHORES += ["%s%d%d" % (_n, _k, _t) for _n in ("ax", "al", "ah") for _k in range(2)]
SEMAPHORES += ["sent", "st"]


def rank_program(g, core, T, topo):
    rank = T.rank_of(core)
    if rank is None:
        return
    n = len(T.cores)
    Q = {"v": g.vector, "a": g.scalar, "p": g.tensor, "g": g, "s": g.sync}
    own = {"v": "qv", "a": "qa", "p": "qp", "g": "qg"}
    count = {}
    known = {q: {} for q in Q}
    wr, rd = {}, {}

    def engines(c):
        return [e for e in topo.engines(c, T.cores[T.rank_of(c) - 1])
                if all(e in topo.engines(c, d) for d in T.cores if d != c)]

    def need(q, ev):
        if ev is None or known[q].get(ev[0], 0) >= ev[1]:
            return
        Q[q].wait_ge(T.sem[ev[0]], ev[1])
        for s, c in list(ev[2].items()) + [(ev[0], ev[1])]:
            if known[q].get(s, 0) < c:
                known[q][s] = c

    def before(q, reads, writes):
        evs = []
        for k in reads:
            evs.append(wr[k])
            if k[0] == "P":
                evs += [e for e in rd.get(k, []) if e[0] != own.get(q)]
        for k in writes:
            evs.append(wr.get(k))
            evs += rd.get(k, [])
        evs = [e for e in evs if e is not None]
        evs.sort(key=lambda e: -e[1])
        for e in evs:
            need(q, e)

    def after(ev, reads, writes):
        for k in reads:
            rd.setdefault(k, []).append(ev)
        for k in writes:
            wr[k] = ev
            rd[k] = []

    def op(q, reads, writes, call):
        before(q, reads, writes)
        s = own[q]
        count[s] = count.get(s, 0) + 1
        call().then_inc(T.sem[s], 1)
        after((s, count[s], dict(known[q])), reads, writes)

    def dma(q, sem, pairs, reads, writes):
        before(q, reads, writes)
        for o, i in pairs:
            Q[q].dma_start(o, i).then_inc(T.sem[sem], 16)
            count[sem] = count.get(sem, 0) + 16
        after((sem, count[sem], dict(known[q])), reads, writes)

    def send(dst, sem, pairs, reads):
        before("g", reads, [])
        rid, pid, _ = topo.addr(dst)
        for o, i in pairs:
            g.remote_dma(o, i, T.sem[sem], T.sem["sent"], pid, rid, sum(1 << e for e in engines(core)))
            count["sent"] = count.get("sent", 0) + len(engines(core))

    def arrives(src, sem, calls, key):
        count[sem] = calls * len(engines(src))
        wr[key] = (sem, count[sem], {})

    V, A, P = g.vector, g.scalar, g.tensor

    def ts(out, in0, s1, o0, s2, o1, reads, writes):
        if o1 is None:
            op("v", reads, writes, lambda: V.tensor_scalar(out, in0, s1, None, o0))
        else:
            op("v", reads, writes, lambda: V.tensor_scalar(out, in0, s1, s2, o0, o1))

    def tt(out, in0, in1, o, reads, writes):
        op("v", reads, writes, lambda: V.tensor_tensor(out, in0, in1, o))

    def cp(out, in_, reads, writes):
        op("v", reads, writes, lambda: V.tensor_copy(out, in_))

    def ms(out, c, key):
        op("v", [], [key], lambda: V.memset(out, c))

    def scan(out, d0, d1, init, o0, o1, reads, writes):
        op("v", reads, writes, lambda: V.tensor_tensor_scan(out, d0, d1, init, o0, o1))

    def quant(q, p, src, reads, writes):
        op("v", reads, writes, lambda: V.quantize_mx(q, p, src))

    def act(out, in_, reads, writes, func=AF.Copy, **kw):
        op("a", reads, writes, lambda: A.activation(out, in_, func, **kw))

    def iota(out, pattern, base, cm, key, flag=True):
        if flag:
            op("g", [], [key], lambda: g.iota(out, pattern, base, cm, allow_small_or_imprecise_dtypes=True))
        else:
            op("g", [], [key], lambda: g.iota(out, pattern, base, cm))

    def mm(out, lq, lp, rq, rp, reads, key):
        op("p", reads, [key], lambda: P.matmul_mx(out, lq, lp, rq, rp, True, True))

    def bank(i, w):
        return (T.p0 if i < 4 else T.p1)[:, 512 * (i % 4):512 * (i % 4) + w]

    def u8(v):
        return v.bitcast(dt.uint8)

    def u32(v):
        return v.bitcast(dt.uint32)

    dma("s", "ldx", [(T.xt[:], T.x[:])], [], ["xt0", "xt1"])
    dma("a", "ldu", [(T.ub[:], T.u[:])], [], ["ub"])
    dma("s", "ldl", [(T.pli[:], T.pl[:])], [], ["pli"])
    dma("s", "ldw", [(u8(T.wq[:, 0:512]), T.wc[:]), (u8(T.wq[:, 512:1024]), T.mc[:]),
                     (T.wp[:, 0:512], T.ws[:]), (T.wp[:, 512:1024], T.ms[:])], [], ["w"])
    dma("s", "ldv", [(T.vb[:], T.v[:])], [], ["vb"])

    def col(i):
        return T.cf[:, i:i + 1]
    W0, W1, W2, U0, U1, U2, U3, TL = range(8)
    M0 = 8
    CP, CQ, S4, S16, TM4, TM7, S4K, TK = range(16, 24)
    iota(T.pi[:], [[0, 1]], 0, 1, "pi", False)
    iota(T.rows[:, 0:8], [[128, 8]], 0, 0, "r128")
    iota(T.rows[:, 32:37], [[4, 5]], -4, 0, "r4")
    iota(T.rows[:, 8:25], [[1, 17]], -1, 0, "r1")
    iota(T.ev[:], [[1, 520]], -3, -4, "ev")
    iota(T.dl[:, 47:ROW - 1], [[0, 7], [-32, 2], [0, 16]], 16, 0, "dl0")
    iota(T.dl[:, ROW + 79:2 * ROW - 1], [[0, 3], [-64, 2], [0, 32]], 32, 0, "dl1")
    iota(T.io4[:], [[4, 256]], 4, 0, "io4")

    ms(T.neg[:], -BIG, "neg")
    ms(T.two[:, 0:16], 2.0, "two")
    ms(T.two[:, 16:32], 1.5, "oh")
    dlk = ["dl0", "dl1"]
    for a, b, c in ((0, 9, 32.0), (9, 15, 16.0), (15, 47, 32.0), (ROW - 1, ROW + 11, 64.0), (ROW + 11, ROW + 15, 32.0),
                    (ROW + 15, ROW + 79, 64.0), (2 * ROW - 1, 2 * ROW, 0.0)):
        act(T.dl[:, a:b], T.neg[:, 0:b - a], ["neg"], ["dlm%d" % a], AF.Identity, scale=0.0, bias=c)
        dlk.append("dlm%d" % a)
    for i, m in enumerate((1, 2, 4, 15, 14, 12, 8, 3)):
        ts(T.ci[:, i:i + 1], T.pi[:], m, ALU.bitwise_and, None, None, ["pi"], ["ci%d" % i])
    cik = ["ci%d" % i for i in range(8)]
    scan(T.hrow[:], T.two[:, 0:16], T.two[:, 16:32], 0.5, ALU.mult, ALU.subtract, ["two", "oh"], ["hrow"])
    cp(T.cf[:, 0:8], T.ci[:], cik, ["cf"])
    ts(T.cf[:, M0:M0 + 8], T.ci[:], -2.0, ALU.mult, None, None, cik, ["cm"])
    act(T.ea[:], T.ev[:], ["ev"], ["ea"], AF.Abs)
    for h in range(2):
        act(T.eb[:, 516 * h:516 * h + 516], T.ea[:, 1 - h:517 - h], ["ea"], ["eb%d" % h], AF.Relu, scale=-1.0, bias=0.5)

    def row(a, b, c=0):
        return T.tab[:, 4 * a + c:4 * b:4]

    def grow(w, c):
        if c is None:
            ts(row(15 + w, 15 + 2 * w), row(15, 15 + w), float(w), ALU.add, None, None, ["t0"], ["t0"])
        else:
            ts(row(15 + w, 15 + 2 * w), row(15, 15 + w), col(c), ALU.add, float(w), ALU.add, ["cm", "cf", "t0"], ["t0"])

    chain = [lambda: ts(row(0, 16), T.two[:, 0:16], 0.0, ALU.mult, col(U0), ALU.add, ["two", "cf"], ["t0"])]
    chain += [lambda w=w, c=c: grow(w, c) for w, c in (
        (1, M0), (2, M0 + 1), (4, M0 + 2), (8, M0 + U3), (16, None), (32, None), (64, None), (128, None),
        (8, U3), (4, U2), (2, U1), (1, U0))]
    loose = [
        lambda: ts(T.uo[:, 0:8], T.rows[:, 0:8], col(U3), ALU.add, 0.125, ALU.mult, ["r128", "cf"], ["uo0"]),
        lambda: ts(T.uo[:, 8:16], T.rows[:, 0:8], 0.125, ALU.mult, 2.0, ALU.add, ["r128"], ["uo1"]),
        lambda: ts(T.tab[:, 0:32:8], T.cf[:, U0:U0 + 4], col(U0), ALU.add, None, None, ["cf", "t0"], ["t1"]),
        lambda: ms(row(ROW - 1, ROW), 0.0, "t2"),
        lambda: ts(col(CQ), col(W2), float(ROW), ALU.mult, 64.0, ALU.add, ["cf"], ["cq"]),
        lambda: ts(col(S4), col(U2), 12.0, ALU.is_equal, 1.0 / KEEP, ALU.max, ["cf"], ["s4"]),
        lambda: ts(col(TK), col(TL), -1024.0, ALU.add, None, None, ["cf"], ["tk"]),
        lambda: tt(col(CP), col(CQ), col(TL), ALU.add, ["cf", "cq"], ["cp"]),
        lambda: ts(T.am[:, 0:4], T.rows[:, 33:37], col(U2), ALU.not_equal, None, None, ["r4", "cf"], ["am0"]),
        lambda: ts(T.am[:, 8:12], T.rows[:, 32:36], col(U2), ALU.is_equal, KEEP - 1.0, ALU.mult, ["r4", "cf"], ["am1"]),
        lambda: ts(T.ao[:, 0:32], T.two[:], 0.0, ALU.mult, col(TL), ALU.add, ["two", "oh", "cf"], ["ao0"]),
        lambda: tt(T.am[:, 16:20], T.am[:, 0:4], T.am[:, 8:12], ALU.add, ["am0", "am1"], ["am2"]),
    ]
    for i in range(len(chain)):
        chain[i]()
        if i < len(loose):
            loose[i]()

    def start(t, h):
        c = slice(128 * h, 128 * h + 128)
        quant(T["xq%d" % t][:, c], T["xp%d" % t][:, c], T.xt[:, 512 * h:512 * h + 512], ["xt%d" % h], ["xq%d%d" % (t, h)])

    def rowlists(t):
        act(T.e4[:], T.ioe[:].indirect(T.plu[:, 32 * t:32 * t + 32]), ["ioe", "plu"], ["e4"])

    def halves(h, s):
        act(T.xw[:, 1024 * s + 512 * h:1024 * s + 512 * h + 512], T.xt[:, 512 * h:512 * h + 512], ["xt%d" % h],
            ["xw%d%d" % (s, h)], scale=0.5 - s)

    act(T.a4[:, 0:256], T.am[:, 16:20].indirect(T.ao[:, 0:16]), ["am2", "ao0"], ["a4"])
    ts(col(S4K), col(S4), 1024.0, ALU.mult, None, None, ["s4"], ["s4k"])
    act(T.ioe[:], T.io4[:], ["io4"], ["ioe"], AF.Identity, scale=1.0 / 1024, bias=-257.0 / 256)
    quant(T.uq[:], T.up[:], T.ub[:], ["ub"], ["uq"])
    start(0, 0)
    start(0, 1)
    cp(u32(T.uq2[:]), u32(T.uq[:]).indirect(T.uo[:]), ["uq", "uo0", "uo1"], ["uq2"])
    act(T.up2[:], T.up[:].indirect(T.uo[:]), ["uq", "uo0", "uo1"], ["up2"])
    cp(T.plu[:], T.pli[:], ["pli"], ["plu"])
    ts(T.am[:, 24:40], T.rows[:, 9:25], col(U0), ALU.not_equal, None, None, ["r1", "cf"], ["am3"])
    ts(T.am[:, 40:56], T.rows[:, 8:24], col(U0), ALU.is_equal, KEEP - 1.0, ALU.mult, ["r1", "cf"], ["am4"])
    ts(T.ao[:, 32:64], T.two[:], 0.0, ALU.mult, col(U0), ALU.add, ["two", "oh", "cf"], ["ao1"])
    tt(T.am[:, 56:72], T.am[:, 24:40], T.am[:, 40:56], ALU.add, ["am3", "am4"], ["am5"])
    rowlists(0)
    act(T.a16[:], T.am[:, 56:72].indirect(T.ao[:, 32:64]), ["am5", "ao1"], ["a16"])
    tt(row(0, ROW, 1), row(0, ROW), T.dl[:, 0:ROW], ALU.add, ["t0", "t1", "t2"] + dlk, ["t3"])
    tt(row(0, ROW, 2), row(0, ROW), T.dl[:, ROW:2 * ROW], ALU.add, ["t0", "t1", "t2"] + dlk, ["t4"])
    tt(row(0, ROW, 3), row(0, ROW, 1), T.dl[:, ROW:2 * ROW], ALU.add, ["t3"] + dlk, ["t5"])
    for a, b, c in ((0, 14, 128.0), (14, 15, 64.0), (15, 143, 128.0), (143, 207, 64.0), (207, ROW, -64.0)):
        q = ["t0", "t1", "t2", "t3", "t4", "t5"]
        if a in (15, 143):
            ts(T.tab[:, HS + 4 * a:HS + 4 * b], T.tab[:, 4 * a:4 * b], c, ALU.add, None, None, q, ["tab%d" % a])
        else:
            act(T.tab[:, HS + 4 * a:HS + 4 * b], T.tab[:, 4 * a:4 * b], q, ["tab%d" % a], AF.Identity, bias=c)
    tabk = ["t0", "t1", "t2", "t3", "t4", "t5"] + ["tab%d" % a for a in (0, 14, 15, 143, 207)]

    def setup3():
        for b in (0, 2, 1, 3):
            o = 516 * (b % 2) + (2 if b < 2 else 0)
            quant(T.eq[:, 128 * b:128 * b + 128], T.ep[:, 128 * b:128 * b + 128], T.eb[:, o:o + 512],
                  ["eb0", "eb1"], ["eq%d" % b])
        ts(col(CQ), col(U0), 15.0, ALU.is_equal, 1.0 / KEEP, ALU.max, ["cf"], ["cq"])
        ts(T.oy[:, 0:64], T.io4[:, 0:256:4], col(U0), ALU.add, -2052.0, ALU.add, ["io4", "cf"], ["oy0"])
        ts(col(TM4), col(TL), -4.0, ALU.add, None, None, ["cf"], ["tm4"])
        ts(col(S16), col(CQ), 256.0, ALU.mult, None, None, ["cq"], ["s16"])
        iota(T.ion[:], [[0, 2], [4, 128]], 4, 0, "ion")
        iota(T.io8[:], [[8, 256]], 8, 0, "io8")
        op("g", ["xt0", "xt1"], ["ma"], lambda: g.affine_select(T.ma[:, 0:2048:2], T.xt[:], [[0, 1024]], ALU.is_ge, -BIG, -1, 0))

    def setup5():
        ts(col(TM7), col(TL), 2.0, ALU.mult, -7.0, ALU.add, ["cf"], ["tm7"])
        cp(T.a4[:, 256:512], T.a4[:, 0:256], ["a4"], ["a4b"])

    for t in range(R):
        lender, borrower = T.cores[(rank + 1 + t) % n], T.cores[(rank - 1 - t) % n]
        xq, xp, lx, lp = T["xq%d" % t], T["xp%d" % t], T["lx%d" % t], T["lp%d" % t]
        hq, hp, lh, lhp = T["hq%d" % t], T["hp%d" % t], T["lh%d" % t], T["lhp%d" % t]
        of, lo = T["of%d" % t], T["lo%d" % t]
        kx, kof, klx, klo = "xq%d" % t, "of%d" % t, "lx%d" % t, "lo%d" % t
        for k in range(2):
            arrives(borrower, "ax%d%d" % (k, t), 2 - k, "%s%d" % (klx, k))
            arrives(borrower, "al%d%d" % (k, t), 1, "%s%d" % (klo, k))
            arrives(lender, "ah%d%d" % (k, t), 2, "lh%d%d" % (k, t))

        send(lender, "ax0%d" % t, [(u8(lx[:, 0:128]), u8(xq[:, 0:128]))], [kx + "0"])
        send(lender, "ax0%d" % t, [(lp[:], xp[:])], [kx + "0", kx + "1"])
        send(lender, "ax1%d" % t, [(u8(lx[:, 128:256]), u8(xq[:, 128:256]))], [kx + "1"])
        for h in range(2):
            c = slice(128 * h, 128 * h + 128)
            for j in range(2):
                mm(bank(4 + 2 * h + j, 128), T.uq2[:, 128 * j:128 * j + 128], T.up2[:, 128 * j:128 * j + 128], xq[:, c], xp[:, c],
                   ["uq2", "up2", "%s%d" % (kx, h)], "P%d" % (4 + 2 * h + j))
        scan(T.run[:, 0:127], T.p1[:, 1:128], T.neg[:, 0:127], -BIG, ALU.max, ALU.max, ["P4", "neg"], ["run"])
        ts(T.tt[:, 0:128], bank(5, 128), 0.0, ALU.is_le, 2.0, ALU.add, ["P5"], ["tt"])
        scan(T.run[:, 127:255], bank(6, 128), T.neg[:, 0:128], T.run[:, 126:127], ALU.max, ALU.max, ["P6", "neg", "run"], ["run"])
        c0, c1 = T.cnt[:, 2 * t:2 * t + 1], T.cnt[:, 2 * t + 1:2 * t + 2]
        act(T.junk[:, 0:255], T.run[:, 0:255], ["run"], ["junk", "c1%d" % t], AF.Sign,
            bias=T.run[:, 254:255], scale=-1.0, accum_out=c1)
        act(T.junk2[:], T.hrow[:], ["hrow", "c1%d" % t], ["junk2", "c0%d" % t], AF.Sign, bias=c1, accum_out=c0)
        ts(T.tt[:, 128:256], bank(7, 128), 0.0, ALU.is_le, 2.0, ALU.add, ["P7"], ["tt2"])

        def places(k):
            c = slice(256 * k, 256 * k + 256)
            tt(T.er[:, c], T.tt[:].indirect(T.plu[:, 32 * t + 16 * k:32 * t + 16 * k + 16]), T.e4[:, c], ALU.add,
               ["tt", "tt2", "plu", "e4"], ["er%d" % k])

        def pairs(k, h, q):
            o = T.gr[:, 256 * k + 128 * h:256 * k + 128 * h + 128]
            i = T.er[:, 256 * k:256 * k + 256].indirect(T.alist[:, 16 * h + 8 * k:16 * h + 8 * k + 8])
            (act if q == "a" else cp)(o, i, ["er%d" % k, "alist"], ["gr%d%d" % (k, h)])

        def offsets(k):
            c = slice(64 * k, 64 * k + 64)
            scan(T.sc[:, 256 * k:256 * k + 256], T.a4[:, 0:256], T.gr[:, 256 * k:256 * k + 256], 0.0, ALU.mult, ALU.max,
                 ["a4", "gr%d0" % k, "gr%d1" % k], ["sc%d" % k])
            ts(of[:, c], T.sc[:, 256 * k + 3:256 * k + 256:4], col(S4K), ALU.mult, col(TK), ALU.add,
               ["sc%d" % k, "s4k", "tk"], ["%s%d" % (kof, k)])
            send(lender, "al%d%d" % (k, t), [(lo[:, c], of[:, c])], ["%s%d" % (kof, k)])

        halves(1, 1)
        places(0)
        ts(T.offu[:], T.cnt[:, 2 * t:2 * t + 2], 4.0, ALU.mult, col(CP), ALU.add, ["c0%d" % t, "c1%d" % t, "cp"], ["offu"])
        cp(T.alist[:], T.tab[:].indirect(T.offu[:]), ["offu"] + tabk, ["alist"])
        pairs(0, 0, "v")
        pairs(0, 1, "a")
        if t == 0:
            halves(0, 1)
            halves(1, 0)
        offsets(0)
        places(1)
        pairs(1, 0, "v")
        pairs(1, 1, "a")
        offsets(1)
        scan(T.sc3[:], T.a4[:, 0:256], T.tt[:], 0.0, ALU.mult, ALU.max, ["a4", "tt", "tt2"], ["sc3"])
        ts(T.oy[:, 64:128], T.sc3[:, 3:256:4], col(S4K), ALU.mult, None, None, ["sc3", "s4k"], ["oy1"])
        guk = []
        for k in range(2):
            for h in range(2):
                guk.append("gu%d%d" % (k, h))
                act(T.gu[:, 256 * k + 128 * h:256 * k + 128 * h + 128],
                    T.e4[:, 256 * k:256 * k + 256].indirect(T.alist[:, 16 * h + 8 * k:16 * h + 8 * k + 8]),
                    ["e4", "alist"], [guk[-1]])
        if t == 0:
            setup3()
        if t == 1:
            quant(T.vq[:], T.vp[:], T.vb[:], ["vb"], ["vq"])

        dwk = []
        for h in range(2):
            c = slice(128 * h, 128 * h + 128)
            for b in (0, 2, 1, 3):
                mm(bank(4 * h + b, 128), T.eq[:, 128 * b:128 * b + 128], T.ep[:, 128 * b:128 * b + 128], lx[:, c], lp[:, c],
                   ["eq%d" % b, klx + "0", "%s%d" % (klx, h)], "P%d" % (4 * h + b))
            for b in range(4):
                for s in range(2):
                    a, key = 1024 * s + 512 * h, "dw%d%d%d" % (s, h, b)
                    dwk.append(key)
                    if b < 2:
                        act(T.dw[:, a + b:a + 512:4], bank(4 * h + b, 128), ["P%d" % (4 * h + b)], [key], scale=1.0 - 2.0 * s)
                    else:
                        ts(T.dw[:, a + b:a + 512:4], bank(4 * h + b, 128), 1.0 - 2.0 * s, ALU.mult, None, None,
                           ["P%d" % (4 * h + b)], [key])

        tt(T.oy[:, 128:192], T.oy[:, 64:128], T.oy[:, 0:64], ALU.add, ["oy0", "oy1"], ["oy2"])
        scan(T.sc2[:], T.a16[:], T.gu[:], 0.0, ALU.mult, ALU.min, ["a16"] + guk, ["sc2"])
        cp(T.ofy[:], T.oy[:, 128:192], ["oy2"], ["ofy"])
        ts(T.l16[:], T.sc2[:, 15:512:16], col(S16), ALU.mult, 256.0, ALU.add, ["sc2", "s16"], ["l16"])

        def zpart(a):
            o = 64 * (a // 512) + a % 512 // 16
            act(T.zi[:, a:a + 256], T.dw[:].indirect(lo[:, o:o + 16]), dwk + ["%s%d" % (klo, a // 512)], ["zi%d" % a])
            tt(T.zt[:, a:a + 256], T.dw[:].indirect(lo[:, o + 32:o + 48]), T.zi[:, a:a + 256], ALU.add,
               dwk + ["%s%d" % (klo, a // 512), "zi%d" % a], ["zt%d" % a])

        def layer(k):
            cols = slice(128 * k, 128 * k + 128)
            quant(T.zq[:, cols], T.zp[:, cols], T.zt[:, 512 * k:512 * k + 512],
                  ["zt%d" % (512 * k), "zt%d" % (512 * k + 256)], ["zq%d" % k])
            for b in range(4):
                i = 4 * (1 - k) + b
                c = slice(512 * k + 128 * b, 512 * k + 128 * b + 128)
                mm(bank(i, 128), T.wq[:, c], T.wp[:, c], T.zq[:, cols], T.zp[:, cols], ["w", "zq%d" % k], "P%d" % i)

        def evac(k, b, q):
            i = 4 * (1 - k) + b
            o = T.ht[:, 512 * k + b:512 * k + 512:4]
            if q == "a":
                act(o, bank(i, 128), ["P%d" % i], ["ht%d%d" % (k, b)], scale=0.03125)
            else:
                ts(o, bank(i, 128), 0.03125, ALU.mult, None, None, ["P%d" % i], ["ht%d%d" % (k, b)])

        def back(k):
            cols = slice(128 * k, 128 * k + 128)
            quant(hq[:, cols], hp[:, cols], T.ht[:, 512 * k:512 * k + 512], ["ht%d%d" % (k, b) for b in range(4)],
                  ["hq%d%d" % (k, t)])
            send(borrower, "ah%d%d" % (k, t), [(u8(lh[:, cols]), u8(hq[:, cols])), (lhp[:, cols], hp[:, cols])],
                 ["hq%d%d" % (k, t)])

        zpart(0)
        zpart(256)
        layer(0)
        zpart(512)
        zpart(768)
        for b in range(4):
            evac(0, b, "a")
        back(0)
        if t == 0:
            halves(0, 0)
        layer(1)
        for b in range(2):
            evac(1, b, "v")
            evac(1, 2 + b, "a")
        back(1)
        if t == 0:
            setup5()

        xwk = ["xw00", "xw01", "xw10", "xw11"]
        cp(T.n1[:].indirect(T.l16[:, 16:32]), T.ion[:], ["l16", "ion"], ["n1"])
        act(T.ys[:], T.xw[:].indirect(of[:, 0:64]), xwk + [kof + "0"], ["ys"])
        act(T.sn[:, 256:512], T.n1[:].indirect(T.l16[:, 0:16]), ["n1", "l16"], ["sn1"])
        cp(T.sn[:, 0:256].indirect(T.l16[:, 0:16]), T.io8[:], ["l16", "io8"], ["sn0"])
        act(T.yn[:], T.xw[:].indirect(T.ofy[:]), xwk + ["ofy"], ["yn"])
        scan(T.sns[:], T.a4[:], T.sn[:], 0.0, ALU.mult, ALU.max, ["a4", "a4b", "sn0", "sn1"], ["sns"])
        ts(T.ofd[:], T.sns[:, 259:512:4], col(S4), ALU.mult, col(TM4), ALU.add, ["sns", "s4", "tm4"], ["ofd"])
        ts(T.off[:], T.sns[:, 3:256:4], col(S4), ALU.mult, col(TM7), ALU.add, ["sns", "s4", "tm7"], ["off"])
        if t == R - 1:
            ts(T.bu[:, 0:3], T.cnt[:, 1:6:2], 1.0, ALU.mult, None, None, ["c1%d" % i for i in range(R)], ["bu"])
            act(T.bg[:], T.io4[:].indirect(T.bu[:, 0:3]), ["bu", "io4"], ["bg"], scale=0.25)
            act(T.bo[:], T.bg[:, 0:48:8], ["bg"], ["bo"])
            dma("s", "st", [(T.od[:], T.bo[0:128:16, :])], ["bo"], [])

        for k in range(2):
            cols = slice(128 * k, 128 * k + 128)
            for b in range(4):
                i = 4 * (1 - k) + b
                mm(bank(i, 128), T.eq[:, 128 * b:128 * b + 128], T.ep[:, 128 * b:128 * b + 128], lh[:, cols], lhp[:, cols],
                   ["eq%d" % b, "lh%d%d" % (k, t)], "P%d" % i)
        mbk = []
        for b in range(4):
            for h in range(2):
                for s, o in ((0, ALU.max), (1, ALU.min)):
                    key = "mb%d%d%d" % (b, h, s)
                    mbk.append(key)
                    tt(T.mb[:, 1024 * h + 2 * b + s:1024 * h + 1024:8], bank(4 + b, 128),
                       T.ys[:, 512 * h + b:512 * h + 512:4], o, ["P%d" % (4 + b), "ys"], [key])
        for b in range(4):
            act(T.d1[:, b:512:4], bank(b, 128), ["P%d" % b], ["d1%d" % b])
        d1k = ["d1%d" % b for b in range(4)] + ["ofd"]
        for q in (1, 2, 3):
            act(T.ma[:, 512 * q + 1:512 * q + 512:2], T.d1[:].indirect(T.ofd[:, 16 * q:16 * q + 16]), d1k, ["ma%d" % q])
        if t < R - 1:
            rowlists(t + 1)
        cp(T.ma[:, 1:512:2], T.d1[:].indirect(T.ofd[:, 0:16]), d1k, ["ma0"])
        for q in (1, 0, 2, 3):
            c = slice(512 * q, 512 * q + 512)
            scan(T.mm[:, c], T.ma[:, c], T.mb[:, c], 0.0, ALU.min, ALU.max, ["ma", "ma%d" % q] + mbk, ["mm%d" % q])
        for h in range(2):
            c = slice(512 * h, 512 * h + 512)
            tt(T.xt[:, c], T.mm[:].indirect(T.off[:, 32 * h:32 * h + 32]), T.yn[:, c], ALU.add,
               ["mm0", "mm1", "mm2", "mm3", "off", "yn"], ["xt%d" % h])
            start(t + 1, h)
            if t < R - 1:
                halves(h, 0)
                if h == 0:
                    halves(0, 1)

    for h in range(2):
        c = slice(128 * h, 128 * h + 128)
        mm(bank(4 + h, 128), T.vq[:], T.vp[:], T.xq3[:, c], T.xp3[:, c], ["vq", "xq3%d" % h], "P%d" % (4 + h))
        dma("s", "st", [(T.oc[:, 512 * h:512 * h + 512], u8(T.xq3[:, c]))], ["xq3%d" % h], [])
        if h:
            dma("s", "st", [(T.osc[4 * k:4 * k + 4, :], T.xp3[32 * k:32 * k + 4, :]) for k in range(4)], ["xq30", "xq31"], [])
        act(T.yo[:, c], bank(4 + h, 128), ["P%d" % (4 + h)], ["yo%d" % h])
        dma("a", "st", [(T.y[:, c], T.yo[:, c])], ["yo%d" % h], [])
    for s in SEMAPHORES:
        if count.get(s, 0) > max(known[q].get(s, 0) for q in Q):
            g.wait_ge(T.sem[s], count[s])
